import numpy as np
import ml_dtypes


def mxq(x, axis, fmt="e4m3"):
    dtype, down = {"e4m3": (ml_dtypes.float8_e4m3fn, 7), "e5m2": (ml_dtypes.float8_e5m2, 14)}[fmt]
    v = np.moveaxis(np.asarray(x, np.float32).astype(ml_dtypes.bfloat16).astype(np.float64), axis, -1)
    blocks = v.reshape(v.shape[:-1] + (-1, 32))
    amax = np.abs(blocks).max(-1, keepdims=True)
    byte = np.maximum(np.where(amax > 0, np.frexp(amax)[1] - 1 + 127, 0) - down, 1)
    scale = np.exp2(byte - 127.0)
    codes = (blocks / scale).astype(np.float32).astype(dtype).astype(np.float64)
    return np.moveaxis((codes * scale).reshape(v.shape), -1, axis)


WIDE = False


def mx_kscale(k):
    if not WIDE:
        return np.ones(k)
    levels = np.array([10, -10, 5, -5, 0])
    if k % 512:
        return np.exp2(np.random.permutation(np.resize(levels, k // 32))).repeat(32)
    a = np.empty((k // 512, 16))
    for p in range(k // 512):
        a[p, :8] = np.random.permutation(np.resize(levels, 8))
        for g in range(8):
            far = levels[np.abs(levels - a[p, g]) >= 10]
            a[p, g + 8] = far[np.random.randint(len(far))]
    return np.exp2(a.ravel()).repeat(32)


def f64(x):
    return np.asarray(x).astype(np.float64)


def striped8(idx):
    return np.asarray(idx).reshape(8, -1, 16).transpose(0, 2, 1).reshape(128, -1).astype(np.uint16)


def unstriped8(offs):
    return offs.reshape(8, 16, -1).transpose(0, 2, 1).reshape(8, -1).astype(np.int64)


def pick8(x, idx, run):
    r = np.arange(len(x))
    return x[r[:, None], idx[r % (8 * run) // run]]


E2M1 = np.array([0.0, 0.5, 1.0, 1.5, 2.0, 3.0, 4.0, 6.0, -0.0, -0.5, -1.0, -1.5, -2.0, -3.0, -4.0, -6.0])


def pack_weight(w, fmt):
    k, n = w.shape
    w = f64(np.asarray(w, np.float32).astype(ml_dtypes.bfloat16)).reshape(k // 32, 32, n)
    amax = np.abs(w).max(1)
    if fmt == "e4m3":
        byte = np.frexp(amax)[1] - 1 + 127 - 7
    else:
        mant, ex = np.frexp(amax / 6.0)
        byte = np.where(mant > 0.5, ex, ex - 1) + 127
    byte = np.clip(np.where(amax > 0, byte, 1), 1, 254)
    scaled = (w * np.exp2(127.0 - byte)[:, None, :]).reshape(k, n).astype(np.float32)
    by_word = np.ascontiguousarray(scaled.reshape(k // 512, 128, 4, n).transpose(0, 1, 3, 2))
    if fmt == "e4m3":
        words = by_word.astype(ml_dtypes.float8_e4m3fn).view(np.uint8)
    else:
        c = by_word.astype(ml_dtypes.float4_e2m1fn).view(np.uint8) & 0xF
        words = (c[..., 0::2] | (c[..., 1::2] << 4)).reshape(k // 512, 128, 2 * n)
    return np.ascontiguousarray(words), np.ascontiguousarray(byte.astype(np.uint8).reshape(k // 512, 16, n))


def unpack_weight(words, scales, fmt):
    g, _, n = scales.shape
    words = np.ascontiguousarray(words).reshape(g, 128, n, -1)
    if fmt == "e4m3":
        vals = words.view(ml_dtypes.float8_e4m3fn).astype(np.float64)
    else:
        nib = np.empty((g, 128, n, 4), np.uint8)
        nib[..., 0::2] = words & 0xF
        nib[..., 1::2] = words >> 4
        vals = E2M1[nib]
    vals = vals * np.repeat(np.exp2(scales.astype(np.float64) - 127.0), 8, axis=1)[..., None]
    return vals.transpose(0, 1, 3, 2).reshape(g * 512, n)


D, T, U, I, O, Q = 512, 1024, 1024, 512, 2048, 128


def setup_inputs():
    n = np.random.standard_normal
    idx = np.stack([np.random.permutation(O)[:I] for _ in range(8)])
    idx2 = np.stack([np.random.permutation(O)[:I] for _ in range(8)])
    idx3 = np.stack([np.random.permutation(O)[:I] for _ in range(8)])
    idx4 = np.stack([np.random.permutation(O)[:I] for _ in range(8)])
    fd = mx_kscale(D)
    cachep = pack_weight(n((D, T)) / fd[:, None], "e2m1")
    draftp = pack_weight(n((D, U)) / fd[:, None], "e4m3")
    return {
        "query": (n((D, Q)) * 1.0 / np.sqrt(D) * fd[:, None]).astype(np.float32),
        "cache_words": cachep[0],
        "cache_scales": cachep[1],
        "draft_words": draftp[0],
        "draft_scales": draftp[1],
        "offs": striped8(idx),
        "offs2": striped8(idx2),
        "offs3": striped8(idx3),
        "offs4": striped8(idx4),
    }


def reference(query, cache_words, cache_scales, draft_words, draft_scales, offs, offs2, offs3, offs4):
    idx = unstriped8(offs)
    idx2 = unstriped8(offs2)
    idx3 = unstriped8(offs3)
    idx4 = unstriped8(offs4)
    cacheu = unpack_weight(cache_words, cache_scales, "e2m1")
    draftu = unpack_weight(draft_words, draft_scales, "e4m3")
    queryq = mxq(f64(query), 0, "e4m3")
    a = queryq.T @ cacheu
    b = queryq.T @ draftu
    ab = np.concatenate([a, b], axis=1)
    f1 = np.zeros((Q, O))
    f1[np.arange(Q)[:, None], idx2[np.arange(Q) % 128 // 16]] = pick8(ab, idx, 16)
    cc = ab + f1
    y = pick8(cc, idx3, 16) - pick8(ab, idx4, 16)
    return y

@@ -1,0 +1,122 @@
+from contextlib import ExitStack
+
+import concourse.mybir as mybir
+
+F32 = mybir.dt.float32
+BF16 = mybir.dt.bfloat16
+I32 = mybir.dt.int32
+U32 = mybir.dt.uint32
+U16 = mybir.dt.uint16
+U8 = mybir.dt.uint8
+FP8X4 = mybir.dt.float8_e4m3fn_x4
+FP4X4 = mybir.dt.float4_e2m1fn_x4
+COPY = mybir.ActivationFunctionType.Copy
+ADD = mybir.AluOpType.add
+SUBTRACT = mybir.AluOpType.subtract
+
+P = 128
+PACK = 4
+Q = 128
+TOKENS = 1024
+PAGE = 2048
+SLOTS = 512
+N = 256
+VECTOR_ADD_BANKS = 6
+
+FLOPS = 2 * 512 * Q * PAGE
+
+
+def load_scale_rows(nc, plane, scales):
+    rows = scales[0].bitcast(I32).rearrange("(h g r) c -> g r h c", h=2, g=2)
+    words = plane[:].bitcast(I32)
+    for g in range(2):
+        nc.sync.dma_start(out=words[32 * g : 32 * g + 4, :].rearrange("r (h c) -> r h c", h=2), in_=rows[g])
+
+
+def spread_scale_rows(nc, plane):
+    words = plane[:].bitcast(I32)
+    half = TOKENS // 4
+    nc.vector.tensor_copy(out=words[64:128, 0:half], in_=words[0:64, half : 2 * half])
+
+
+def tile_attend_endtoend_two_kernel(tc, query, cache_words, cache_scales, draft_words, draft_scales, offs, offs2, offs3, offs4, out):
+    nc = tc.nc
+    with ExitStack() as ctx:
+        lists = ctx.enter_context(tc.tile_pool(name="lists", bufs=1))
+        keep = ctx.enter_context(tc.tile_pool(name="keep", bufs=1))
+        psum = ctx.enter_context(tc.psum_pool(name="psum", bufs=1))
+
+        cache_plane = keep.tile([P, 2 * TOKENS], U8, align_bytes=64)
+        draft_plane = keep.tile([P, 2 * TOKENS], U8, align_bytes=64)
+        nc.vector.memset(cache_plane[:].bitcast(I32)[0:64, :], 0)
+        nc.gpsimd.memset(draft_plane[:].bitcast(I32)[0:64, :], 0)
+
+        q_raw = keep.tile([P, PACK, Q], F32)
+        nc.sync.dma_start(out=q_raw[:], in_=query.rearrange("(p j) q -> p j q", j=PACK))
+        cache_codes = keep.tile([P, 2 * TOKENS], U8, align_bytes=64)
+        nc.sync.dma_start(out=cache_codes[:].bitcast(I32), in_=cache_words[0].bitcast(I32))
+        load_scale_rows(nc, cache_plane, cache_scales)
+        load_scale_rows(nc, draft_plane, draft_scales)
+        draft_rows = draft_words[0].rearrange("p n t -> p (n t)").bitcast(I32)
+        draft_codes = []
+        for h in range(2):
+            codes = keep.tile([P, TOKENS // 2], I32, name="draft_codes%d" % h, align_bytes=64)
+            nc.sync.dma_start(out=codes[:], in_=draft_rows[:, h * (TOKENS // 2) : (h + 1) * (TOKENS // 2)])
+            draft_codes.append(codes)
+
+        offsets = []
+        for name, source in (("pick", offs), ("put", offs2), ("plain", offs4), ("read", offs3)):
+            held = lists.tile([P, SLOTS // 16], U16, name=name)
+            nc.sync.dma_start(held[:], source)
+            offsets.append(held)
+        pick, put, plain, read = offsets
+
+        f1 = keep.tile([P, PAGE], F32)
+        nc.vector.memset(f1[:], 0.0)
+
+        grouped = keep.tile([P, Q, PACK], BF16, align_bytes=64)
+        nc.vector.tensor_copy(
+            out=grouped[:].rearrange("p (c i) t -> p c t i", i=4),
+            in_=q_raw[:].rearrange("p t (c i) -> p c t i", i=4),
+        )
+        spread_scale_rows(nc, cache_plane)
+        q_codes = keep.tile([P, Q], U32, align_bytes=64)
+        q_scales = keep.tile([P, Q], U8, align_bytes=64)
+        nc.vector.quantize_mx(out=q_codes[:].bitcast(FP8X4), scales=q_scales[:], in_=grouped[:].rearrange("p q t -> p (q t)"))
+        spread_scale_rows(nc, draft_plane)
+
+        ab = keep.tile([P, PAGE], F32)
+        banks = []
+        for b in range(PAGE // N):
+            bank = psum.tile([P, N], F32, name="bank%d" % b)
+            first = (b * N) % TOKENS
+            if b * N < TOKENS:
+                keys = cache_codes[:, 2 * first : 2 * (first + N)].bitcast(FP4X4)
+                key_scales = cache_plane[:, first : first + N]
+            else:
+                inside = first % (TOKENS // 2)
+                keys = draft_codes[first // (TOKENS // 2)][:, inside : inside + N].bitcast(FP8X4)
+                key_scales = draft_plane[:, first : first + N]
+            nc.tensor.matmul_mx(out=bank[:], lhsT=q_codes[:].bitcast(FP8X4), lhsT_scale=q_scales[:], rhs=keys, rhs_scale=key_scales, start=True, stop=True)
+            if b % 2 == 0:
+                nc.scalar.activation(ab[:, b * N : (b + 1) * N], bank[:], COPY)
+            else:
+                nc.vector.tensor_copy(out=ab[:, b * N : (b + 1) * N], in_=bank[:])
+            banks.append(bank)
+
+        picked = keep.tile([P, SLOTS], F32)
+        nc.vector.tensor_copy(picked[:], ab[:].indirect(pick[:]))
+        nc.scalar.activation(f1[:].indirect(put[:]), picked[:], COPY)
+        subtrahend = keep.tile([P, SLOTS], F32)
+        nc.vector.tensor_copy(subtrahend[:], ab[:].indirect(plain[:]))
+
+        cc = keep.tile([P, PAGE], F32)
+        rest = slice(VECTOR_ADD_BANKS * N, PAGE)
+        nc.gpsimd.tensor_tensor(cc[:, rest], f1[:, rest], ab[:, rest], ADD)
+        for b in range(VECTOR_ADD_BANKS):
+            cols = slice(b * N, (b + 1) * N)
+            nc.vector.tensor_tensor(cc[:, cols], f1[:, cols], banks[b][:], ADD)
+
+        result = keep.tile([P, SLOTS], F32)
+        nc.vector.tensor_tensor(result[:], cc[:].indirect(read[:]), subtrahend[:], SUBTRACT)
+        nc.sync.dma_start(out=out, in_=result[:])

@@ -20,23 +20,12 @@ Q = 128
 TOKENS = 1024
 PAGE = 2048
 SLOTS = 512
-N = 256
-VECTOR_ADD_BANKS = 6
+WIDTHS = (256, 256, 512, 256, 256, 256, 128, 128)
+ON_VECTOR = (3, 4, 6)
+VECTOR_ADD_COLUMNS = 1408
+DRAFT_ROW = 4
 
 FLOPS = 2 * 512 * Q * PAGE
-
-
-def load_scale_rows(nc, plane, scales):
-    rows = scales[0].bitcast(I32).rearrange("(h g r) c -> g r h c", h=2, g=2)
-    words = plane[:].bitcast(I32)
-    for g in range(2):
-        nc.sync.dma_start(out=words[32 * g : 32 * g + 4, :].rearrange("r (h c) -> r h c", h=2), in_=rows[g])
-
-
-def spread_scale_rows(nc, plane):
-    words = plane[:].bitcast(I32)
-    half = TOKENS // 4
-    nc.vector.tensor_copy(out=words[64:128, 0:half], in_=words[0:64, half : 2 * half])
 
 
 def tile_attend_endtoend_two_kernel(tc, query, cache_words, cache_scales, draft_words, draft_scales, offs, offs2, offs3, offs4, out):
@@ -46,23 +35,26 @@ def tile_attend_endtoend_two_kernel(tc, query, cache_words, cache_scales, draft_
         keep = ctx.enter_context(tc.tile_pool(name="keep", bufs=1))
         psum = ctx.enter_context(tc.psum_pool(name="psum", bufs=1))
 
-        cache_plane = keep.tile([P, 2 * TOKENS], U8, align_bytes=64)
-        draft_plane = keep.tile([P, 2 * TOKENS], U8, align_bytes=64)
-        nc.vector.memset(cache_plane[:].bitcast(I32)[0:64, :], 0)
-        nc.gpsimd.memset(draft_plane[:].bitcast(I32)[0:64, :], 0)
+        cache_plane = keep.tile([P, TOKENS], U8, align_bytes=64)
+        draft_plane = keep.tile([P, 4 * TOKENS], U8, align_bytes=64)
+        cache_plane_words = cache_plane[:].bitcast(I32)
+        draft_plane_words = draft_plane[:].bitcast(I32)
+        nc.vector.memset(cache_plane_words, 0)
+        nc.vector.memset(draft_plane_words[0:32, :], 0)
 
         q_raw = keep.tile([P, PACK, Q], F32)
         nc.sync.dma_start(out=q_raw[:], in_=query.rearrange("(p j) q -> p j q", j=PACK))
         cache_codes = keep.tile([P, 2 * TOKENS], U8, align_bytes=64)
         nc.sync.dma_start(out=cache_codes[:].bitcast(I32), in_=cache_words[0].bitcast(I32))
-        load_scale_rows(nc, cache_plane, cache_scales)
-        load_scale_rows(nc, draft_plane, draft_scales)
-        draft_rows = draft_words[0].rearrange("p n t -> p (n t)").bitcast(I32)
-        draft_codes = []
-        for h in range(2):
-            codes = keep.tile([P, TOKENS // 2], I32, name="draft_codes%d" % h, align_bytes=64)
-            nc.sync.dma_start(out=codes[:], in_=draft_rows[:, h * (TOKENS // 2) : (h + 1) * (TOKENS // 2)])
-            draft_codes.append(codes)
+        cache_rows = cache_scales[0].bitcast(I32)
+        for g in range(4):
+            nc.sync.dma_start(out=cache_plane_words[32 * g : 32 * g + 4, :], in_=cache_rows[4 * g : 4 * g + 4, :])
+        nc.sync.dma_start(
+            out=draft_plane_words[DRAFT_ROW : DRAFT_ROW + 4, :].rearrange("r (g c) -> r g c", g=4),
+            in_=draft_scales[0].bitcast(I32).rearrange("(g r) c -> r g c", g=4),
+        )
+        draft_codes = keep.tile([P, TOKENS], I32, align_bytes=64)
+        nc.sync.dma_start(out=draft_codes[:], in_=draft_words[0].rearrange("p n t -> p (n t)").bitcast(I32))
 
         offsets = []
         for name, source in (("pick", offs), ("put", offs2), ("plain", offs4), ("read", offs3)):
@@ -79,30 +71,32 @@ def tile_attend_endtoend_two_kernel(tc, query, cache_words, cache_scales, draft_
             out=grouped[:].rearrange("p (c i) t -> p c t i", i=4),
             in_=q_raw[:].rearrange("p t (c i) -> p c t i", i=4),
         )
-        spread_scale_rows(nc, cache_plane)
         q_codes = keep.tile([P, Q], U32, align_bytes=64)
         q_scales = keep.tile([P, Q], U8, align_bytes=64)
         nc.vector.quantize_mx(out=q_codes[:].bitcast(FP8X4), scales=q_scales[:], in_=grouped[:].rearrange("p q t -> p (q t)"))
-        spread_scale_rows(nc, draft_plane)
+        row = TOKENS // 4
+        for g in range(1, 4):
+            nc.vector.tensor_copy(out=draft_plane_words[32 * g : 32 * g + 32, 0:row], in_=draft_plane_words[0:32, g * row : (g + 1) * row])
 
         ab = keep.tile([P, PAGE], F32)
         banks = []
-        for b in range(PAGE // N):
-            bank = psum.tile([P, N], F32, name="bank%d" % b)
-            first = (b * N) % TOKENS
-            if b * N < TOKENS:
-                keys = cache_codes[:, 2 * first : 2 * (first + N)].bitcast(FP4X4)
-                key_scales = cache_plane[:, first : first + N]
+        start = 0
+        for b, n in enumerate(WIDTHS):
+            bank = psum.tile([P, n], F32, name="bank%d" % b)
+            first = start % TOKENS
+            if start < TOKENS:
+                keys = cache_codes[:, 2 * first : 2 * (first + n)].bitcast(FP4X4)
+                key_scales = cache_plane[:, first : first + n]
             else:
-                inside = first % (TOKENS // 2)
-                keys = draft_codes[first // (TOKENS // 2)][:, inside : inside + N].bitcast(FP8X4)
-                key_scales = draft_plane[:, first : first + N]
+                keys = draft_codes[:, first : first + n].bitcast(FP8X4)
+                key_scales = draft_plane[DRAFT_ROW:P, first : first + n]
             nc.tensor.matmul_mx(out=bank[:], lhsT=q_codes[:].bitcast(FP8X4), lhsT_scale=q_scales[:], rhs=keys, rhs_scale=key_scales, start=True, stop=True)
-            if b % 2 == 0:
-                nc.scalar.activation(ab[:, b * N : (b + 1) * N], bank[:], COPY)
+            if b in ON_VECTOR:
+                nc.vector.tensor_copy(out=ab[:, start : start + n], in_=bank[:])
             else:
-                nc.vector.tensor_copy(out=ab[:, b * N : (b + 1) * N], in_=bank[:])
-            banks.append(bank)
+                nc.scalar.activation(ab[:, start : start + n], bank[:], COPY)
+            banks.append((start, n, bank))
+            start += n
 
         picked = keep.tile([P, SLOTS], F32)
         nc.vector.tensor_copy(picked[:], ab[:].indirect(pick[:]))
@@ -111,11 +105,13 @@ def tile_attend_endtoend_two_kernel(tc, query, cache_words, cache_scales, draft_
         nc.vector.tensor_copy(subtrahend[:], ab[:].indirect(plain[:]))
 
         cc = keep.tile([P, PAGE], F32)
-        rest = slice(VECTOR_ADD_BANKS * N, PAGE)
+        rest = slice(VECTOR_ADD_COLUMNS, PAGE)
         nc.gpsimd.tensor_tensor(cc[:, rest], f1[:, rest], ab[:, rest], ADD)
-        for b in range(VECTOR_ADD_BANKS):
-            cols = slice(b * N, (b + 1) * N)
-            nc.vector.tensor_tensor(cc[:, cols], f1[:, cols], banks[b][:], ADD)
+        for start, n, bank in banks:
+            mine = min(n, VECTOR_ADD_COLUMNS - start)
+            if mine > 0:
+                cols = slice(start, start + mine)
+                nc.vector.tensor_tensor(cc[:, cols], f1[:, cols], bank[:, 0:mine], ADD)
 
         result = keep.tile([P, SLOTS], F32)
         nc.vector.tensor_tensor(result[:], cc[:].indirect(read[:]), subtrahend[:], SUBTRACT)

from contextlib import ExitStack

import concourse.mybir as mybir

F32 = mybir.dt.float32
BF16 = mybir.dt.bfloat16
I32 = mybir.dt.int32
U32 = mybir.dt.uint32
U16 = mybir.dt.uint16
U8 = mybir.dt.uint8
FP8X4 = mybir.dt.float8_e4m3fn_x4
FP4X4 = mybir.dt.float4_e2m1fn_x4
COPY = mybir.ActivationFunctionType.Copy
ADD = mybir.AluOpType.add
SUBTRACT = mybir.AluOpType.subtract

P = 128
PACK = 4
Q = 128
TOKENS = 1024
PAGE = 2048
SLOTS = 512
WIDTHS = (256, 256, 512, 256, 256, 256, 128, 128)
ON_VECTOR = (3, 4, 6)
VECTOR_ADD_COLUMNS = 1408
DRAFT_ROW = 4

FLOPS = 2 * 512 * Q * PAGE


def tile_attend_endtoend_two_kernel(tc, query, cache_words, cache_scales, draft_words, draft_scales, offs, offs2, offs3, offs4, out):
    nc = tc.nc
    with ExitStack() as ctx:
        lists = ctx.enter_context(tc.tile_pool(name="lists", bufs=1))
        keep = ctx.enter_context(tc.tile_pool(name="keep", bufs=1))
        psum = ctx.enter_context(tc.psum_pool(name="psum", bufs=1))

        cache_plane = keep.tile([P, TOKENS], U8, align_bytes=64)
        draft_plane = keep.tile([P, 4 * TOKENS], U8, align_bytes=64)
        cache_plane_words = cache_plane[:].bitcast(I32)
        draft_plane_words = draft_plane[:].bitcast(I32)
        nc.vector.memset(cache_plane_words, 0)
        nc.vector.memset(draft_plane_words[0:32, :], 0)

        q_raw = keep.tile([P, PACK, Q], F32)
        nc.sync.dma_start(out=q_raw[:], in_=query.rearrange("(p j) q -> p j q", j=PACK))
        cache_codes = keep.tile([P, 2 * TOKENS], U8, align_bytes=64)
        nc.sync.dma_start(out=cache_codes[:].bitcast(I32), in_=cache_words[0].bitcast(I32))
        cache_rows = cache_scales[0].bitcast(I32)
        for g in range(4):
            nc.sync.dma_start(out=cache_plane_words[32 * g : 32 * g + 4, :], in_=cache_rows[4 * g : 4 * g + 4, :])
        nc.sync.dma_start(
            out=draft_plane_words[DRAFT_ROW : DRAFT_ROW + 4, :].rearrange("r (g c) -> r g c", g=4),
            in_=draft_scales[0].bitcast(I32).rearrange("(g r) c -> r g c", g=4),
        )
        draft_codes = keep.tile([P, TOKENS], I32, align_bytes=64)
        nc.sync.dma_start(out=draft_codes[:], in_=draft_words[0].rearrange("p n t -> p (n t)").bitcast(I32))

        offsets = []
        for name, source in (("pick", offs), ("put", offs2), ("plain", offs4), ("read", offs3)):
            held = lists.tile([P, SLOTS // 16], U16, name=name)
            nc.sync.dma_start(held[:], source)
            offsets.append(held)
        pick, put, plain, read = offsets

        f1 = keep.tile([P, PAGE], F32)
        nc.vector.memset(f1[:], 0.0)

        grouped = keep.tile([P, Q, PACK], BF16, align_bytes=64)
        nc.vector.tensor_copy(
            out=grouped[:].rearrange("p (c i) t -> p c t i", i=4),
            in_=q_raw[:].rearrange("p t (c i) -> p c t i", i=4),
        )
        q_codes = keep.tile([P, Q], U32, align_bytes=64)
        q_scales = keep.tile([P, Q], U8, align_bytes=64)
        nc.vector.quantize_mx(out=q_codes[:].bitcast(FP8X4), scales=q_scales[:], in_=grouped[:].rearrange("p q t -> p (q t)"))
        row = TOKENS // 4
        for g in range(1, 4):
            nc.vector.tensor_copy(out=draft_plane_words[32 * g : 32 * g + 32, 0:row], in_=draft_plane_words[0:32, g * row : (g + 1) * row])

        ab = keep.tile([P, PAGE], F32)
        banks = []
        start = 0
        for b, n in enumerate(WIDTHS):
            bank = psum.tile([P, n], F32, name="bank%d" % b)
            first = start % TOKENS
            if start < TOKENS:
                keys = cache_codes[:, 2 * first : 2 * (first + n)].bitcast(FP4X4)
                key_scales = cache_plane[:, first : first + n]
            else:
                keys = draft_codes[:, first : first + n].bitcast(FP8X4)
                key_scales = draft_plane[DRAFT_ROW:P, first : first + n]
            nc.tensor.matmul_mx(out=bank[:], lhsT=q_codes[:].bitcast(FP8X4), lhsT_scale=q_scales[:], rhs=keys, rhs_scale=key_scales, start=True, stop=True)
            if b in ON_VECTOR:
                nc.vector.tensor_copy(out=ab[:, start : start + n], in_=bank[:])
            else:
                nc.scalar.activation(ab[:, start : start + n], bank[:], COPY)
            banks.append((start, n, bank))
            start += n

        picked = keep.tile([P, SLOTS], F32)
        nc.vector.tensor_copy(picked[:], ab[:].indirect(pick[:]))
        nc.scalar.activation(f1[:].indirect(put[:]), picked[:], COPY)
        subtrahend = keep.tile([P, SLOTS], F32)
        nc.vector.tensor_copy(subtrahend[:], ab[:].indirect(plain[:]))

        cc = keep.tile([P, PAGE], F32)
        rest = slice(VECTOR_ADD_COLUMNS, PAGE)
        nc.gpsimd.tensor_tensor(cc[:, rest], f1[:, rest], ab[:, rest], ADD)
        for start, n, bank in banks:
            mine = min(n, VECTOR_ADD_COLUMNS - start)
            if mine > 0:
                cols = slice(start, start + mine)
                nc.vector.tensor_tensor(cc[:, cols], f1[:, cols], bank[:, 0:mine], ADD)

        result = keep.tile([P, SLOTS], F32)
        nc.vector.tensor_tensor(result[:], cc[:].indirect(read[:]), subtrahend[:], SUBTRACT)
        nc.sync.dma_start(out=out, in_=result[:])
